import numpy as np
import ml_dtypes


def mxq(x, axis, fmt="e4m3"):
    dtype, down = {"e4m3": (ml_dtypes.float8_e4m3fn, 7), "e5m2": (ml_dtypes.float8_e5m2, 14)}[fmt]
    v = np.moveaxis(np.asarray(x, np.float32).astype(ml_dtypes.bfloat16).astype(np.float64), axis, -1)
    blocks = v.reshape(v.shape[:-1] + (-1, 32))
    amax = np.abs(blocks).max(-1, keepdims=True)
    byte = np.maximum(np.where(amax > 0, np.frexp(amax)[1] - 1 + 127, 0) - down, 1)
    scale = np.exp2(byte - 127.0)
    codes = (blocks / scale).astype(np.float32).astype(dtype).astype(np.float64)
    return np.moveaxis((codes * scale).reshape(v.shape), -1, axis)


WIDE = False


def mx_kscale(k):
    if not WIDE:
        return np.ones(k)
    levels = np.array([10, -10, 5, -5, 0])
    if k % 512:
        return np.exp2(np.random.permutation(np.resize(levels, k // 32))).repeat(32)
    a = np.empty((k // 512, 16))
    for p in range(k // 512):
        a[p, :8] = np.random.permutation(np.resize(levels, 8))
        for g in range(8):
            far = levels[np.abs(levels - a[p, g]) >= 10]
            a[p, g + 8] = far[np.random.randint(len(far))]
    return np.exp2(a.ravel()).repeat(32)


def f64(x):
    return np.asarray(x).astype(np.float64)


def striped(idx):
    return np.tile(idx.reshape(-1, 16).T, (8, 1)).astype(np.uint16)


def unstriped(offs):
    return offs[:16].T.reshape(-1).astype(np.int64)


def striped8(idx):
    return np.concatenate([x.reshape(-1, 16).T for x in idx]).astype(np.uint16)


def runs(offs, k):
    lists = np.stack([offs[16 * r : 16 * r + 16].T.reshape(-1) for r in range(8)]).astype(np.int64)
    return lists[np.arange(k) % 512 // 64]


def pack_weight(w):
    k, n = w.shape
    w = f64(np.asarray(w, np.float32).astype(ml_dtypes.bfloat16)).reshape(k // 32, 32, n)
    amax = np.abs(w).max(1)
    byte = np.clip(np.where(amax > 0, np.frexp(amax)[1] - 1 + 127 - 7, 1), 1, 254)
    scaled = (w * np.exp2(127.0 - byte)[:, None, :]).reshape(k, n).astype(np.float32)
    words = np.ascontiguousarray(scaled.reshape(k // 512, 128, 4, n).transpose(0, 1, 3, 2)).astype(ml_dtypes.float8_e4m3fn).view(np.uint8)
    return words, np.ascontiguousarray(byte.astype(np.uint8).reshape(k // 512, 16, n))


def unpack_weight(words, scales):
    g, p, n, _ = words.shape
    vals = np.ascontiguousarray(words).view(ml_dtypes.float8_e4m3fn).astype(np.float64) * np.repeat(np.exp2(scales.astype(np.float64) - 127.0), 8, axis=1)[..., None]
    return vals.transpose(0, 1, 3, 2).reshape(g * 512, n)


def sigmoid(v):
    return 1.0 / (1.0 + np.exp(-np.maximum(v, -700.0)))


K, T, S, N, H, W, U = 512, 2048, 512, 512, 512, 256, 1024


def setup_inputs():
    n = np.random.standard_normal
    s = mx_kscale(K)[:, None]
    u = mx_kscale(S)
    packed_xT = pack_weight(n((K, T)) * s)
    perm = np.stack([np.random.permutation(H) for _ in range(8)])
    return {
        "x_words": packed_xT[0],
        "x_scales": packed_xT[1],
        "wa": (n((K, H)) / np.sqrt(K) / s).astype(np.float32),
        "wb": (n((K, N)) / np.sqrt(K) / s).astype(np.float32),
        "gt": (np.random.uniform(0.5, 1.5, (S, 1)) * u[:, None]).astype(np.float32),
        "gi": (np.random.uniform(0.5, 1.5, (S, 1)) / u[:, None]).astype(np.float32),
        "mem": n((H, U)).astype(np.float32),
        "offs": striped(np.random.permutation(T)[:S]),
        "two": striped(np.random.permutation(T)[:S]),
        "n1": striped8(perm[:, :W]),
        "n2": striped8(perm[:, W:]),
        "n3": striped8(np.stack([np.random.permutation(U)[:N] for _ in range(8)])),
    }


def reference(x_words, x_scales, wa, wb, gt, gi, mem, offs, two, n1, n2, n3):
    old = f64(mem)[np.arange(H)[:, None], runs(n3, H)]
    xq = unpack_weight(x_words, x_scales)[:, unstriped(offs)]
    a = xq.T @ mxq(f64(wa), 0, "e4m3")
    pa = a[np.arange(S)[:, None], runs(n1, S)]
    pb = a[np.arange(S)[:, None], runs(n2, S)]
    ra = pa * sigmoid(pb)
    ds = a.copy()
    ds[np.arange(S)[:, None], runs(n2, S)] = ra
    z = f64(gt) * ds
    x_two = unpack_weight(x_words, x_scales)[:, unstriped(two)]
    b = x_two.T @ mxq(f64(wb), 0, "e4m3")
    z2 = f64(gi) * b
    cv = 0.0625 * ((mxq(z, 0, "e4m3").T @ mxq(z2, 0, "e4m3")))
    nw = old + sigmoid(cv) * (cv - old)
    out = f64(mem).copy()
    out[np.arange(H)[:, None], runs(n3, H)] = nw
    return out

@@ -1,0 +1,211 @@
+from contextlib import ExitStack
+
+import concourse.mybir as mybir
+from concourse.masks import make_identity
+
+K, T, S, N, H, W, U = 512, 2048, 512, 512, 512, 256, 1024
+FLOPS = 2 * K * S * H + 2 * K * S * N + 2 * S * H * N
+
+F32 = mybir.dt.float32
+BF16 = mybir.dt.bfloat16
+I32 = mybir.dt.int32
+U32 = mybir.dt.uint32
+U16 = mybir.dt.uint16
+U8 = mybir.dt.uint8
+FP8X4 = mybir.dt.float8_e4m3fn_x4
+ACT = mybir.ActivationFunctionType
+ALU = mybir.AluOpType
+
+P = 128
+PACK = 4
+
+
+def tile_picked_momfoldpaget_none_p_kernel(tc, x_words, x_scales, wa, wb, gt, gi, mem, offs, two, n1, n2, n3, out):
+    nc = tc.nc
+    with ExitStack() as ctx:
+        keep = ctx.enter_context(tc.tile_pool(name="keep", bufs=1))
+        psum = ctx.enter_context(tc.psum_pool(name="psum", bufs=1))
+
+        def sb(name, shape, dtype, tag=None):
+            return keep.tile(shape, dtype, name=name, tag=tag or name, align_bytes=64)
+
+        def bank(i):
+            return psum.tile([P, 512], F32, name="bank%d" % i)
+
+        def load_list(name, src):
+            t = keep.tile(list(src.shape), U16, name=name)
+            nc.sync.dma_start(t[:], src)
+            return t
+
+        def weave(engine, dst, src):
+            o = dst.rearrange("p (c i) t -> p c t i", i=4)
+            s = src.rearrange("p t (c i) -> p c t i", i=4)
+            if engine == "scalar":
+                nc.scalar.copy(o, s)
+            else:
+                nc.vector.tensor_copy(o, s)
+
+        def quantize(codes, scales, src):
+            nc.vector.quantize_mx(out=codes.bitcast(FP8X4), scales=scales, in_=src.rearrange("p c t -> p (c t)"))
+
+        xs = sb("xs", [P, T], U8)
+        nc.gpsimd.memset(xs[:].bitcast(I32), 0)
+        for q in range(4):
+            nc.scalar.dma_start(xs[32 * q : 32 * q + 4, :].bitcast(I32), x_scales[0, 4 * q : 4 * q + 4, :].bitcast(I32))
+        ident = sb("ident", [P, P], F32)
+        make_identity(nc, ident[:])
+        grow = sb("grow", [P, P], F32)
+        nc.gpsimd.memset(grow[:], 0.0)
+        warm = sb("warm", [P, 1], F32)
+        nc.scalar.activation(warm[:], ident[:, 0:1], ACT.Sigmoid)
+
+        offs_t = load_list("offs_t", offs)
+        xw = sb("xw", [P, T], I32)
+        nc.sync.dma_start(xw[:], x_words[0].rearrange("p n t -> p (n t)").bitcast(I32))
+        two_t = load_list("two_t", two)
+        n2_t = load_list("n2_t", n2)
+        n1_t = load_list("n1_t", n1)
+        n3_t = load_list("n3_t", n3)
+        w_raw = []
+        for name, w, tags in (("wa", wa, (None, None)), ("wb", wb, (None, None))):
+            for h in range(2):
+                half = sb("%s_raw%d" % (name, h), [P, PACK, 256], F32, tag=tags[h])
+                nc.sync.dma_start(half[:], w.rearrange("(p j) c -> p j c", j=PACK)[:, :, 256 * h : 256 * h + 256])
+                w_raw.append(half)
+
+        for r, g in enumerate((gt, gi)):
+            nc.sync.dma_start(
+                grow[4 * r : 4 * r + 4, :].rearrange("t (q e) -> t q e", e=8),
+                g.rearrange("(q t e) o -> t q (e o)", t=4, e=8),
+            )
+
+        def pick_bytes(name, lst, tag=None):
+            raw = sb(name + "_raw", [P, S], U8, tag=tag)
+            nc.vector.tensor_copy(raw[:], xs[:].indirect(lst[:]))
+            dealt = sb(name, [P, S], U8)
+            nc.vector.tensor_copy(
+                dealt[:].bitcast(I32).rearrange("p (t q e) -> p t q e", t=4, e=2),
+                raw[:].bitcast(I32).rearrange("p (q t e) -> p t q e", t=4, e=2),
+            )
+            return dealt
+
+        def pick_words(name, lst):
+            words = sb(name, [P, S], U32)
+            nc.vector.tensor_copy(
+                words[:].rearrange("p (t q e) -> p q t e", t=4, e=8),
+                xw[:].bitcast(U32).indirect(lst[:]),
+            )
+            return words
+
+        xa_w = pick_words("xa_w", offs_t)
+        xb_w = pick_words("xb_w", two_t)
+        xa_s = pick_bytes("xa_s", offs_t)
+
+        w16, w_c, w_s = [], [], []
+        for i, name in enumerate(("wa", "wb")):
+            w_c.append(sb(name + "_c", [P, H], U32))
+            w_s.append(sb(name + "_s", [P, H], U8))
+            for h in range(2):
+                half = sb("%s16_%d" % (name, h), [P, 256, PACK], BF16)
+                weave("scalar", half[:], w_raw[2 * i + h][:])
+                w16.append(half)
+        for h in range(2):
+            cols = slice(256 * h, 256 * h + 256)
+            quantize(w_c[0][:, cols], w_s[0][:, cols], w16[h][:])
+        xb_s = pick_bytes("xb_s", two_t, tag="wa16_1")
+        for h in range(2):
+            cols = slice(256 * h, 256 * h + 256)
+            quantize(w_c[1][:, cols], w_s[1][:, cols], w16[2 + h][:])
+
+        page = []
+        mem_v = mem.rearrange("(p t) w -> t p w", t=PACK)
+        out_v = out.rearrange("(p t) w -> t p w", t=PACK)
+        for t, tag in enumerate(("wa_raw0", "wa_raw1", "wb_raw0", "wa16_0")):
+            pg = sb("page%d" % t, [P, U], F32, tag=tag)
+            nc.sync.dma_start(pg[:], mem_v[t])
+            page.append(pg)
+
+        def product(i, lhs_c, lhs_s, t, rhs_c, rhs_s):
+            acc = bank(i)
+            cols = slice(P * t, P * t + P)
+            nc.tensor.matmul_mx(
+                out=acc[:],
+                lhsT=lhs_c[:, cols].bitcast(FP8X4),
+                lhsT_scale=lhs_s[:, cols],
+                rhs=rhs_c[:].bitcast(FP8X4),
+                rhs_scale=rhs_s[:],
+                start=True,
+                stop=True,
+            )
+            return acc
+
+        a_sb, sig = [], []
+        for t in range(PACK):
+            acc = product(t, xa_w, xa_s, t, w_c[0], w_s[0])
+            a_t = sb("a%d" % t, [P, H], F32, tag="wb_raw1" if t == 0 else None)
+            nc.scalar.copy(a_t[:], acc[:])
+            s_t = sb("sig%d" % t, [P, W], F32)
+            nc.scalar.activation(s_t[:], a_t[:].indirect(n2_t[:]), ACT.Sigmoid)
+            a_sb.append(a_t)
+            sig.append(s_t)
+
+        gbank = bank(7)
+        nc.tensor.transpose(gbank[:, 0:P], grow[:], ident[:])
+        gates = sb("gates", [P, 8], F32)
+        nc.scalar.copy(gates[:], gbank[:, 0:8])
+
+        pa = []
+        for t in range(PACK):
+            pa.append(sb("pa%d" % t, [P, W], F32))
+        nc.vector.tensor_copy(pa[0][:], a_sb[0][:].indirect(n1_t[:]))
+
+        z2_rows = sb("z2_rows", [P, PACK, N], BF16)
+        for t in range(PACK):
+            acc = product(4 + t, xb_w, xb_s, t, w_c[1], w_s[1])
+            nc.scalar.activation(z2_rows[:, t, :], acc[:], ACT.Copy, scale=gates[:, 4 + t : 5 + t])
+
+        z_rows = None
+        z2_16 = sb("z2_16", [P, N, PACK], BF16)
+        for t in range(PACK):
+            if t + 1 < PACK:
+                nc.vector.tensor_copy(pa[t + 1][:], a_sb[t + 1][:].indirect(n1_t[:]))
+            nc.vector.tensor_tensor(a_sb[t][:].indirect(n2_t[:]), pa[t][:], sig[t][:], ALU.mult)
+            if t == 0:
+                weave("scalar", z2_16[:], z2_rows[:])
+                z_rows = sb("z_rows", [P, PACK, H], BF16, tag="z2_rows")
+            nc.scalar.activation(
+                z_rows[:, t, :].rearrange("p (u m) -> p m u", u=PACK),
+                a_sb[t][:].rearrange("p (m u) -> p m u", u=PACK),
+                ACT.Copy,
+                scale=gates[:, t : t + 1],
+            )
+
+        z2_c = sb("z2_c", [P, N], U32)
+        z2_s = sb("z2_s", [P, N], U8)
+        quantize(z2_c[:], z2_s[:], z2_16[:])
+
+        z16 = sb("z16", [P, H, PACK], BF16)
+        z_c = sb("z_c", [P, H], U32)
+        z_s = sb("z_s", [P, H], U8)
+        for u in range(PACK + 1):
+            if u < PACK:
+                cols = slice(P * u, P * u + P)
+                weave("vector", z16[:, cols, :], z_rows[:, :, cols])
+            if u > 0:
+                cols = slice(P * (u - 1), P * u)
+                quantize(z_c[:, cols], z_s[:, cols], z16[:, cols, :])
+
+        accs, kept = [], []
+        for u in range(PACK):
+            acc = product(u, z_c, z_s, u, z2_c, z2_s)
+            rest = sb("rest%d" % u, [P, N], F32)
+            nc.scalar.activation(rest[:], acc[:], ACT.Sigmoid, scale=-0.0625)
+            k_u = sb("kept%d" % u, [P, N], F32, tag="z16" if u == 0 else None)
+            nc.vector.tensor_tensor(k_u[:], page[u][:].indirect(n3_t[:]), rest[:], ALU.mult)
+            accs.append(acc)
+            kept.append(k_u)
+        for u in range(PACK):
+            fresh = sb("fresh%d" % u, [P, N], F32, tag="z_c" if u == 0 else None)
+            nc.scalar.activation(fresh[:], accs[u][:], ACT.Silu, scale=0.0625)
+            nc.vector.tensor_tensor(page[u][:].indirect(n3_t[:]), kept[u][:], fresh[:], ALU.add)
+            nc.sync.dma_start(out_v[u], page[u][:])

@@ -52,32 +52,29 @@ def tile_picked_momfoldpaget_none_p_kernel(tc, x_words, x_scales, wa, wb, gt, gi
         nc.gpsimd.memset(xs[:].bitcast(I32), 0)
         for q in range(4):
             nc.scalar.dma_start(xs[32 * q : 32 * q + 4, :].bitcast(I32), x_scales[0, 4 * q : 4 * q + 4, :].bitcast(I32))
+        cold = sb("cold", [P, 1], F32)
+        nc.gpsimd.memset(cold[:], 0.0)
+        warm = sb("warm", [P, 1], F32)
+        nc.scalar.activation(warm[:], cold[:], ACT.Sigmoid)
+
         ident = sb("ident", [P, P], F32)
         make_identity(nc, ident[:])
-        grow = sb("grow", [P, P], F32)
-        nc.gpsimd.memset(grow[:], 0.0)
-        warm = sb("warm", [P, 1], F32)
-        nc.scalar.activation(warm[:], ident[:, 0:1], ACT.Sigmoid)
-
         offs_t = load_list("offs_t", offs)
-        xw = sb("xw", [P, T], I32)
-        nc.sync.dma_start(xw[:], x_words[0].rearrange("p n t -> p (n t)").bitcast(I32))
         two_t = load_list("two_t", two)
         n2_t = load_list("n2_t", n2)
         n1_t = load_list("n1_t", n1)
-        n3_t = load_list("n3_t", n3)
+        xw = sb("xw", [P, T], I32)
+        nc.sync.dma_start(xw[:], x_words[0].rearrange("p n t -> p (n t)").bitcast(I32))
         w_raw = []
-        for name, w, tags in (("wa", wa, (None, None)), ("wb", wb, (None, None))):
-            for h in range(2):
-                half = sb("%s_raw%d" % (name, h), [P, PACK, 256], F32, tag=tags[h])
-                nc.sync.dma_start(half[:], w.rearrange("(p j) c -> p j c", j=PACK)[:, :, 256 * h : 256 * h + 256])
-                w_raw.append(half)
-
-        for r, g in enumerate((gt, gi)):
-            nc.sync.dma_start(
-                grow[4 * r : 4 * r + 4, :].rearrange("t (q e) -> t q e", e=8),
-                g.rearrange("(q t e) o -> t q (e o)", t=4, e=8),
-            )
+        for h in range(2):
+            half = sb("wa_raw%d" % h, [P, PACK, 256], F32)
+            nc.sync.dma_start(half[:], wa.rearrange("(p j) c -> p j c", j=PACK)[:, :, 256 * h : 256 * h + 256])
+            w_raw.append(half[:])
+        n3_t = load_list("n3_t", n3)
+        for h, tag in enumerate(("warm", "cold")):
+            half = sb("wb_raw%d" % h, [P, PACK, 256], F32, tag=tag)
+            nc.sync.dma_start(half[:], wb.rearrange("(p j) c -> p j c", j=PACK)[:, :, 256 * h : 256 * h + 256])
+            w_raw.append(half[:])
 
         def pick_bytes(name, lst, tag=None):
             raw = sb(name + "_raw", [P, S], U8, tag=tag)
@@ -107,7 +104,7 @@ def tile_picked_momfoldpaget_none_p_kernel(tc, x_words, x_scales, wa, wb, gt, gi
             w_s.append(sb(name + "_s", [P, H], U8))
             for h in range(2):
                 half = sb("%s16_%d" % (name, h), [P, 256, PACK], BF16)
-                weave("scalar", half[:], w_raw[2 * i + h][:])
+                weave("scalar", half[:], w_raw[2 * i + h])
                 w16.append(half)
         for h in range(2):
             cols = slice(256 * h, 256 * h + 256)
@@ -117,10 +114,17 @@ def tile_picked_momfoldpaget_none_p_kernel(tc, x_words, x_scales, wa, wb, gt, gi
             cols = slice(256 * h, 256 * h + 256)
             quantize(w_c[1][:, cols], w_s[1][:, cols], w16[2 + h][:])
 
+        grow = sb("grow", [P, P], F32, tag="wa_raw0")
+        nc.gpsimd.memset(grow[:], 0.0)
+        for r, g in enumerate((gt, gi)):
+            nc.sync.dma_start(
+                grow[4 * r : 4 * r + 4, :].rearrange("t (q e) -> t q e", e=8),
+                g.rearrange("(q t e) o -> t q (e o)", t=4, e=8),
+            )
         page = []
         mem_v = mem.rearrange("(p t) w -> t p w", t=PACK)
         out_v = out.rearrange("(p t) w -> t p w", t=PACK)
-        for t, tag in enumerate(("wa_raw0", "wa_raw1", "wb_raw0", "wa16_0")):
+        for t, tag in enumerate(("xw", "wa_raw1", "wa16_0", "xa_s_raw")):
             pg = sb("page%d" % t, [P, U], F32, tag=tag)
             nc.sync.dma_start(pg[:], mem_v[t])
             page.append(pg)
@@ -139,46 +143,60 @@ def tile_picked_momfoldpaget_none_p_kernel(tc, x_words, x_scales, wa, wb, gt, gi
             )
             return acc
 
-        a_sb, sig = [], []
-        for t in range(PACK):
-            acc = product(t, xa_w, xa_s, t, w_c[0], w_s[0])
-            a_t = sb("a%d" % t, [P, H], F32, tag="wb_raw1" if t == 0 else None)
-            nc.scalar.copy(a_t[:], acc[:])
+        a_acc = [product(t, xa_w, xa_s, t, w_c[0], w_s[0]) for t in range(PACK)]
+        a_sb, sig, pa = [], [], []
+
+        def leave_bank(t, tag):
+            a_t = sb("a%d" % t, [P, H], F32, tag=tag)
+            nc.scalar.copy(a_t[:], a_acc[t][:])
             s_t = sb("sig%d" % t, [P, W], F32)
             nc.scalar.activation(s_t[:], a_t[:].indirect(n2_t[:]), ACT.Sigmoid)
             a_sb.append(a_t)
             sig.append(s_t)
 
-        gbank = bank(7)
+        def fetch(t):
+            p_t = sb("pa%d" % t, [P, W], F32)
+            nc.vector.tensor_copy(p_t[:], a_sb[t][:].indirect(n1_t[:]))
+            pa.append(p_t)
+
+        def put(t):
+            nc.vector.tensor_tensor(a_sb[t][:].indirect(n2_t[:]), pa[t][:], sig[t][:], ALU.mult)
+
+        z_rows = sb("z_rows", [P, PACK, H], BF16)
+
+        def weigh(t):
+            nc.vector.tensor_scalar_mul(
+                z_rows[:, t, :].rearrange("p (u m) -> p m u", u=PACK),
+                a_sb[t][:].rearrange("p (m u) -> p m u", u=PACK),
+                gates[:, t : t + 1],
+            )
+
+        leave_bank(0, "warm")
+        leave_bank(1, "cold")
+        gbank = bank(0)
         nc.tensor.transpose(gbank[:, 0:P], grow[:], ident[:])
         gates = sb("gates", [P, 8], F32)
         nc.scalar.copy(gates[:], gbank[:, 0:8])
 
-        pa = []
-        for t in range(PACK):
-            pa.append(sb("pa%d" % t, [P, W], F32))
-        nc.vector.tensor_copy(pa[0][:], a_sb[0][:].indirect(n1_t[:]))
+        leave_bank(2, "wb16_1")
+        fetch(0)
+        fetch(1)
+        put(0)
+        leave_bank(3, "pa0")
 
         z2_rows = sb("z2_rows", [P, PACK, N], BF16)
         for t in range(PACK):
             acc = product(4 + t, xb_w, xb_s, t, w_c[1], w_s[1])
             nc.scalar.activation(z2_rows[:, t, :], acc[:], ACT.Copy, scale=gates[:, 4 + t : 5 + t])
-
-        z_rows = None
         z2_16 = sb("z2_16", [P, N, PACK], BF16)
-        for t in range(PACK):
+        weave("scalar", z2_16[:], z2_rows[:])
+
+        for t in range(1, PACK):
             if t + 1 < PACK:
-                nc.vector.tensor_copy(pa[t + 1][:], a_sb[t + 1][:].indirect(n1_t[:]))
-            nc.vector.tensor_tensor(a_sb[t][:].indirect(n2_t[:]), pa[t][:], sig[t][:], ALU.mult)
-            if t == 0:
-                weave("scalar", z2_16[:], z2_rows[:])
-                z_rows = sb("z_rows", [P, PACK, H], BF16, tag="z2_rows")
-            nc.scalar.activation(
-                z_rows[:, t, :].rearrange("p (u m) -> p m u", u=PACK),
-                a_sb[t][:].rearrange("p (m u) -> p m u", u=PACK),
-                ACT.Copy,
-                scale=gates[:, t : t + 1],
-            )
+                fetch(t + 1)
+            put(t)
+            weigh(t - 1)
+        weigh(PACK - 1)
 
         z2_c = sb("z2_c", [P, N], U32)
         z2_s = sb("z2_s", [P, N], U8)
@@ -204,8 +222,8 @@ def tile_picked_momfoldpaget_none_p_kernel(tc, x_words, x_scales, wa, wb, gt, gi
             nc.vector.tensor_tensor(k_u[:], page[u][:].indirect(n3_t[:]), rest[:], ALU.mult)
             accs.append(acc)
             kept.append(k_u)
+        fresh = sb("fresh", [P, PACK, N], F32, tag="z_c")
         for u in range(PACK):
-            fresh = sb("fresh%d" % u, [P, N], F32, tag="z_c" if u == 0 else None)
-            nc.scalar.activation(fresh[:], accs[u][:], ACT.Silu, scale=0.0625)
-            nc.vector.tensor_tensor(page[u][:].indirect(n3_t[:]), kept[u][:], fresh[:], ALU.add)
+            nc.scalar.activation(fresh[:, u, :], accs[u][:], ACT.Silu, scale=0.0625)
+            nc.vector.tensor_tensor(page[u][:].indirect(n3_t[:]), kept[u][:], fresh[:, u, :], ALU.add)
             nc.sync.dma_start(out_v[u], page[u][:])

@@ -48,28 +48,27 @@ def tile_picked_momfoldpaget_none_p_kernel(tc, x_words, x_scales, wa, wb, gt, gi
         def quantize(codes, scales, src):
             nc.vector.quantize_mx(out=codes.bitcast(FP8X4), scales=scales, in_=src.rearrange("p c t -> p (c t)"))
 
-        xs = sb("xs", [P, T], U8)
-        nc.gpsimd.memset(xs[:].bitcast(I32), 0)
-        for q in range(4):
-            nc.scalar.dma_start(xs[32 * q : 32 * q + 4, :].bitcast(I32), x_scales[0, 4 * q : 4 * q + 4, :].bitcast(I32))
         cold = sb("cold", [P, 1], F32)
         nc.gpsimd.memset(cold[:], 0.0)
         warm = sb("warm", [P, 1], F32)
         nc.scalar.activation(warm[:], cold[:], ACT.Sigmoid)
-
+        xs = sb("xs", [P, T], U8)
+        nc.gpsimd.memset(xs[:].bitcast(I32), 0)
         ident = sb("ident", [P, P], F32)
         make_identity(nc, ident[:])
         offs_t = load_list("offs_t", offs)
         two_t = load_list("two_t", two)
         n2_t = load_list("n2_t", n2)
-        n1_t = load_list("n1_t", n1)
         xw = sb("xw", [P, T], I32)
         nc.sync.dma_start(xw[:], x_words[0].rearrange("p n t -> p (n t)").bitcast(I32))
+        for q in range(4):
+            nc.sync.dma_start(xs[32 * q : 32 * q + 4, :].bitcast(I32), x_scales[0, 4 * q : 4 * q + 4, :].bitcast(I32))
         w_raw = []
         for h in range(2):
             half = sb("wa_raw%d" % h, [P, PACK, 256], F32)
             nc.sync.dma_start(half[:], wa.rearrange("(p j) c -> p j c", j=PACK)[:, :, 256 * h : 256 * h + 256])
             w_raw.append(half[:])
+        n1_t = load_list("n1_t", n1)
         n3_t = load_list("n3_t", n3)
         for h, tag in enumerate(("warm", "cold")):
             half = sb("wb_raw%d" % h, [P, PACK, 256], F32, tag=tag)
@@ -99,20 +98,25 @@ def tile_picked_momfoldpaget_none_p_kernel(tc, x_words, x_scales, wa, wb, gt, gi
         xa_s = pick_bytes("xa_s", offs_t)
 
         w16, w_c, w_s = [], [], []
-        for i, name in enumerate(("wa", "wb")):
+        for name in ("wa", "wb"):
             w_c.append(sb(name + "_c", [P, H], U32))
             w_s.append(sb(name + "_s", [P, H], U8))
-            for h in range(2):
-                half = sb("%s16_%d" % (name, h), [P, 256, PACK], BF16)
-                weave("scalar", half[:], w_raw[2 * i + h])
-                w16.append(half)
-        for h in range(2):
-            cols = slice(256 * h, 256 * h + 256)
-            quantize(w_c[0][:, cols], w_s[0][:, cols], w16[h][:])
-        xb_s = pick_bytes("xb_s", two_t, tag="wa16_1")
-        for h in range(2):
-            cols = slice(256 * h, 256 * h + 256)
-            quantize(w_c[1][:, cols], w_s[1][:, cols], w16[2 + h][:])
+
+        def round_half(j, tag=None):
+            half = sb("w16_%d" % j, [P, 256, PACK], BF16, tag=tag)
+            weave("scalar", half[:], w_raw[j])
+            w16.append(half)
+
+        def quantize_half(j):
+            cols = slice(256 * (j % 2), 256 * (j % 2) + 256)
+            quantize(w_c[j // 2][:, cols], w_s[j // 2][:, cols], w16[j][:])
+
+        for j in range(3):
+            round_half(j)
+        quantize_half(0)
+        quantize_half(1)
+        xb_s = pick_bytes("xb_s", two_t, tag="w16_1")
+        quantize_half(2)
 
         grow = sb("grow", [P, P], F32, tag="wa_raw0")
         nc.gpsimd.memset(grow[:], 0.0)
@@ -124,7 +128,7 @@ def tile_picked_momfoldpaget_none_p_kernel(tc, x_words, x_scales, wa, wb, gt, gi
         page = []
         mem_v = mem.rearrange("(p t) w -> t p w", t=PACK)
         out_v = out.rearrange("(p t) w -> t p w", t=PACK)
-        for t, tag in enumerate(("xw", "wa_raw1", "wa16_0", "xa_s_raw")):
+        for t, tag in enumerate(("xw", "wa_raw1", "w16_0", "xa_s_raw")):
             pg = sb("page%d" % t, [P, U], F32, tag=tag)
             nc.sync.dma_start(pg[:], mem_v[t])
             page.append(pg)
@@ -146,12 +150,14 @@ def tile_picked_momfoldpaget_none_p_kernel(tc, x_words, x_scales, wa, wb, gt, gi
         a_acc = [product(t, xa_w, xa_s, t, w_c[0], w_s[0]) for t in range(PACK)]
         a_sb, sig, pa = [], [], []
 
-        def leave_bank(t, tag):
+        def leave_bank(t, tag=None):
             a_t = sb("a%d" % t, [P, H], F32, tag=tag)
             nc.scalar.copy(a_t[:], a_acc[t][:])
-            s_t = sb("sig%d" % t, [P, W], F32)
-            nc.scalar.activation(s_t[:], a_t[:].indirect(n2_t[:]), ACT.Sigmoid)
             a_sb.append(a_t)
+
+        def gate(t):
+            s_t = sb("sig%d" % t, [P, W], F32)
+            nc.scalar.activation(s_t[:], a_sb[t][:].indirect(n2_t[:]), ACT.Sigmoid)
             sig.append(s_t)
 
         def fetch(t):
@@ -162,8 +168,6 @@ def tile_picked_momfoldpaget_none_p_kernel(tc, x_words, x_scales, wa, wb, gt, gi
         def put(t):
             nc.vector.tensor_tensor(a_sb[t][:].indirect(n2_t[:]), pa[t][:], sig[t][:], ALU.mult)
 
-        z_rows = sb("z_rows", [P, PACK, H], BF16)
-
         def weigh(t):
             nc.vector.tensor_scalar_mul(
                 z_rows[:, t, :].rearrange("p (u m) -> p m u", u=PACK),
@@ -171,18 +175,24 @@ def tile_picked_momfoldpaget_none_p_kernel(tc, x_words, x_scales, wa, wb, gt, gi
                 gates[:, t : t + 1],
             )
 
-        leave_bank(0, "warm")
-        leave_bank(1, "cold")
+        leave_bank(0)
+        leave_bank(1)
+        gate(0)
+        gate(1)
+        round_half(3, "xa_w")
+        fetch(0)
+        fetch(1)
+        put(0)
+        put(1)
+        quantize_half(3)
+        leave_bank(2, "cold")
+        leave_bank(3, "pa0")
+        gate(2)
+        gate(3)
         gbank = bank(0)
         nc.tensor.transpose(gbank[:, 0:P], grow[:], ident[:])
         gates = sb("gates", [P, 8], F32)
         nc.scalar.copy(gates[:], gbank[:, 0:8])
-
-        leave_bank(2, "wb16_1")
-        fetch(0)
-        fetch(1)
-        put(0)
-        leave_bank(3, "pa0")
 
         z2_rows = sb("z2_rows", [P, PACK, N], BF16)
         for t in range(PACK):
@@ -191,18 +201,21 @@ def tile_picked_momfoldpaget_none_p_kernel(tc, x_words, x_scales, wa, wb, gt, gi
         z2_16 = sb("z2_16", [P, N, PACK], BF16)
         weave("scalar", z2_16[:], z2_rows[:])
 
-        for t in range(1, PACK):
-            if t + 1 < PACK:
-                fetch(t + 1)
-            put(t)
-            weigh(t - 1)
-        weigh(PACK - 1)
+        z_rows = sb("z_rows", [P, PACK, H], BF16, tag="pa1")
+        fetch(2)
+        fetch(3)
+        weigh(0)
+        put(2)
+        weigh(1)
+        put(3)
+        weigh(2)
 
         z2_c = sb("z2_c", [P, N], U32)
         z2_s = sb("z2_s", [P, N], U8)
         quantize(z2_c[:], z2_s[:], z2_16[:])
+        weigh(PACK - 1)
 
-        z16 = sb("z16", [P, H, PACK], BF16)
+        z16 = sb("z16", [P, H, PACK], BF16, tag="z2_16")
         z_c = sb("z_c", [P, H], U32)
         z_s = sb("z_s", [P, H], U8)
         for u in range(PACK + 1):
@@ -218,7 +231,7 @@ def tile_picked_momfoldpaget_none_p_kernel(tc, x_words, x_scales, wa, wb, gt, gi
             acc = product(u, z_c, z_s, u, z2_c, z2_s)
             rest = sb("rest%d" % u, [P, N], F32)
             nc.scalar.activation(rest[:], acc[:], ACT.Sigmoid, scale=-0.0625)
-            k_u = sb("kept%d" % u, [P, N], F32, tag="z16" if u == 0 else None)
+            k_u = sb("kept%d" % u, [P, N], F32, tag="z2_16" if u == 0 else None)
             nc.vector.tensor_tensor(k_u[:], page[u][:].indirect(n3_t[:]), rest[:], ALU.mult)
             accs.append(acc)
             kept.append(k_u)

@@ -111,12 +111,11 @@ def tile_picked_momfoldpaget_none_p_kernel(tc, x_words, x_scales, wa, wb, gt, gi
             cols = slice(256 * (j % 2), 256 * (j % 2) + 256)
             quantize(w_c[j // 2][:, cols], w_s[j // 2][:, cols], w16[j][:])
 
-        for j in range(3):
+        for j in range(2):
             round_half(j)
         quantize_half(0)
         quantize_half(1)
         xb_s = pick_bytes("xb_s", two_t, tag="w16_1")
-        quantize_half(2)
 
         grow = sb("grow", [P, P], F32, tag="wa_raw0")
         nc.gpsimd.memset(grow[:], 0.0)
@@ -179,14 +178,16 @@ def tile_picked_momfoldpaget_none_p_kernel(tc, x_words, x_scales, wa, wb, gt, gi
         leave_bank(1)
         gate(0)
         gate(1)
-        round_half(3, "xa_w")
+        wb16 = sb("wb16", [P, N, PACK], BF16, tag="xa_w")
+        for h in range(2):
+            weave("scalar", wb16[:, 256 * h : 256 * h + 256, :], w_raw[2 + h])
         fetch(0)
         fetch(1)
         put(0)
         put(1)
-        quantize_half(3)
-        leave_bank(2, "cold")
-        leave_bank(3, "pa0")
+        quantize(w_c[1][:], w_s[1][:], wb16[:])
+        leave_bank(2, "warm")
+        leave_bank(3, "cold")
         gate(2)
         gate(3)
         gbank = bank(0)
@@ -198,8 +199,11 @@ def tile_picked_momfoldpaget_none_p_kernel(tc, x_words, x_scales, wa, wb, gt, gi
         for t in range(PACK):
             acc = product(4 + t, xb_w, xb_s, t, w_c[1], w_s[1])
             nc.scalar.activation(z2_rows[:, t, :], acc[:], ACT.Copy, scale=gates[:, 4 + t : 5 + t])
-        z2_16 = sb("z2_16", [P, N, PACK], BF16)
-        weave("scalar", z2_16[:], z2_rows[:])
+        z2_16 = []
+        for h in range(2):
+            half = sb("z2_16_%d" % h, [P, 256, PACK], BF16)
+            weave("scalar", half[:], z2_rows[:, :, 256 * h : 256 * h + 256])
+            z2_16.append(half)
 
         z_rows = sb("z_rows", [P, PACK, H], BF16, tag="pa1")
         fetch(2)
@@ -212,10 +216,12 @@ def tile_picked_momfoldpaget_none_p_kernel(tc, x_words, x_scales, wa, wb, gt, gi
 
         z2_c = sb("z2_c", [P, N], U32)
         z2_s = sb("z2_s", [P, N], U8)
-        quantize(z2_c[:], z2_s[:], z2_16[:])
         weigh(PACK - 1)
+        for h in range(2):
+            cols = slice(256 * h, 256 * h + 256)
+            quantize(z2_c[:, cols], z2_s[:, cols], z2_16[h][:])
 
-        z16 = sb("z16", [P, H, PACK], BF16, tag="z2_16")
+        z16 = sb("z16", [P, H, PACK], BF16, tag="z2_16_0")
         z_c = sb("z_c", [P, H], U32)
         z_s = sb("z_s", [P, H], U8)
         for u in range(PACK + 1):
@@ -231,7 +237,7 @@ def tile_picked_momfoldpaget_none_p_kernel(tc, x_words, x_scales, wa, wb, gt, gi
             acc = product(u, z_c, z_s, u, z2_c, z2_s)
             rest = sb("rest%d" % u, [P, N], F32)
             nc.scalar.activation(rest[:], acc[:], ACT.Sigmoid, scale=-0.0625)
-            k_u = sb("kept%d" % u, [P, N], F32, tag="z2_16" if u == 0 else None)
+            k_u = sb("kept%d" % u, [P, N], F32, tag="z2_16_0" if u == 0 else None)
             nc.vector.tensor_tensor(k_u[:], page[u][:].indirect(n3_t[:]), rest[:], ALU.mult)
             accs.append(acc)
             kept.append(k_u)

@@ -58,9 +58,9 @@ def tile_picked_momfoldpaget_none_p_kernel(tc, x_words, x_scales, wa, wb, gt, gi
         make_identity(nc, ident[:])
         offs_t = load_list("offs_t", offs)
         two_t = load_list("two_t", two)
-        n2_t = load_list("n2_t", n2)
         xw = sb("xw", [P, T], I32)
         nc.sync.dma_start(xw[:], x_words[0].rearrange("p n t -> p (n t)").bitcast(I32))
+        n2_t = load_list("n2_t", n2)
         for q in range(4):
             nc.sync.dma_start(xs[32 * q : 32 * q + 4, :].bitcast(I32), x_scales[0, 4 * q : 4 * q + 4, :].bitcast(I32))
         w_raw = []
@@ -168,11 +168,12 @@ def tile_picked_momfoldpaget_none_p_kernel(tc, x_words, x_scales, wa, wb, gt, gi
             nc.vector.tensor_tensor(a_sb[t][:].indirect(n2_t[:]), pa[t][:], sig[t][:], ALU.mult)
 
         def weigh(t):
-            nc.vector.tensor_scalar_mul(
-                z_rows[:, t, :].rearrange("p (u m) -> p m u", u=PACK),
-                a_sb[t][:].rearrange("p (m u) -> p m u", u=PACK),
-                gates[:, t : t + 1],
-            )
+            dst = z_rows[:, t, :].rearrange("p (u m) -> p m u", u=PACK)
+            src = a_sb[t][:].rearrange("p (m u) -> p m u", u=PACK)
+            if t == 0:
+                nc.scalar.activation(dst, src, ACT.Copy, scale=gates[:, t : t + 1])
+            else:
+                nc.vector.tensor_scalar_mul(dst, src, gates[:, t : t + 1])
 
         leave_bank(0)
         leave_bank(1)
@@ -209,8 +210,8 @@ def tile_picked_momfoldpaget_none_p_kernel(tc, x_words, x_scales, wa, wb, gt, gi
         fetch(2)
         fetch(3)
         weigh(0)
-        put(2)
         weigh(1)
+        put(2)
         put(3)
         weigh(2)
 

from contextlib import ExitStack

import concourse.mybir as mybir
from concourse.masks import make_identity

K, T, S, N, H, W, U = 512, 2048, 512, 512, 512, 256, 1024
FLOPS = 2 * K * S * H + 2 * K * S * N + 2 * S * H * N

F32 = mybir.dt.float32
BF16 = mybir.dt.bfloat16
I32 = mybir.dt.int32
U32 = mybir.dt.uint32
U16 = mybir.dt.uint16
U8 = mybir.dt.uint8
FP8X4 = mybir.dt.float8_e4m3fn_x4
ACT = mybir.ActivationFunctionType
ALU = mybir.AluOpType

P = 128
PACK = 4


def tile_picked_momfoldpaget_none_p_kernel(tc, x_words, x_scales, wa, wb, gt, gi, mem, offs, two, n1, n2, n3, out):
    nc = tc.nc
    with ExitStack() as ctx:
        keep = ctx.enter_context(tc.tile_pool(name="keep", bufs=1))
        psum = ctx.enter_context(tc.psum_pool(name="psum", bufs=1))

        def sb(name, shape, dtype, tag=None):
            return keep.tile(shape, dtype, name=name, tag=tag or name, align_bytes=64)

        def bank(i):
            return psum.tile([P, 512], F32, name="bank%d" % i)

        def load_list(name, src):
            t = keep.tile(list(src.shape), U16, name=name)
            nc.sync.dma_start(t[:], src)
            return t

        def weave(engine, dst, src):
            o = dst.rearrange("p (c i) t -> p c t i", i=4)
            s = src.rearrange("p t (c i) -> p c t i", i=4)
            if engine == "scalar":
                nc.scalar.copy(o, s)
            else:
                nc.vector.tensor_copy(o, s)

        def quantize(codes, scales, src):
            nc.vector.quantize_mx(out=codes.bitcast(FP8X4), scales=scales, in_=src.rearrange("p c t -> p (c t)"))

        cold = sb("cold", [P, 1], F32)
        nc.gpsimd.memset(cold[:], 0.0)
        warm = sb("warm", [P, 1], F32)
        nc.scalar.activation(warm[:], cold[:], ACT.Sigmoid)
        xs = sb("xs", [P, T], U8)
        nc.gpsimd.memset(xs[:].bitcast(I32), 0)
        ident = sb("ident", [P, P], F32)
        make_identity(nc, ident[:])
        offs_t = load_list("offs_t", offs)
        two_t = load_list("two_t", two)
        xw = sb("xw", [P, T], I32)
        nc.sync.dma_start(xw[:], x_words[0].rearrange("p n t -> p (n t)").bitcast(I32))
        n2_t = load_list("n2_t", n2)
        for q in range(4):
            nc.sync.dma_start(xs[32 * q : 32 * q + 4, :].bitcast(I32), x_scales[0, 4 * q : 4 * q + 4, :].bitcast(I32))
        w_raw = []
        for h in range(2):
            half = sb("wa_raw%d" % h, [P, PACK, 256], F32)
            nc.sync.dma_start(half[:], wa.rearrange("(p j) c -> p j c", j=PACK)[:, :, 256 * h : 256 * h + 256])
            w_raw.append(half[:])
        n1_t = load_list("n1_t", n1)
        n3_t = load_list("n3_t", n3)
        for h, tag in enumerate(("warm", "cold")):
            half = sb("wb_raw%d" % h, [P, PACK, 256], F32, tag=tag)
            nc.sync.dma_start(half[:], wb.rearrange("(p j) c -> p j c", j=PACK)[:, :, 256 * h : 256 * h + 256])
            w_raw.append(half[:])

        def pick_bytes(name, lst, tag=None):
            raw = sb(name + "_raw", [P, S], U8, tag=tag)
            nc.vector.tensor_copy(raw[:], xs[:].indirect(lst[:]))
            dealt = sb(name, [P, S], U8)
            nc.vector.tensor_copy(
                dealt[:].bitcast(I32).rearrange("p (t q e) -> p t q e", t=4, e=2),
                raw[:].bitcast(I32).rearrange("p (q t e) -> p t q e", t=4, e=2),
            )
            return dealt

        def pick_words(name, lst):
            words = sb(name, [P, S], U32)
            nc.vector.tensor_copy(
                words[:].rearrange("p (t q e) -> p q t e", t=4, e=8),
                xw[:].bitcast(U32).indirect(lst[:]),
            )
            return words

        xa_w = pick_words("xa_w", offs_t)
        xb_w = pick_words("xb_w", two_t)
        xa_s = pick_bytes("xa_s", offs_t)

        w16, w_c, w_s = [], [], []
        for name in ("wa", "wb"):
            w_c.append(sb(name + "_c", [P, H], U32))
            w_s.append(sb(name + "_s", [P, H], U8))

        def round_half(j, tag=None):
            half = sb("w16_%d" % j, [P, 256, PACK], BF16, tag=tag)
            weave("scalar", half[:], w_raw[j])
            w16.append(half)

        def quantize_half(j):
            cols = slice(256 * (j % 2), 256 * (j % 2) + 256)
            quantize(w_c[j // 2][:, cols], w_s[j // 2][:, cols], w16[j][:])

        for j in range(2):
            round_half(j)
        quantize_half(0)
        quantize_half(1)
        xb_s = pick_bytes("xb_s", two_t, tag="w16_1")

        grow = sb("grow", [P, P], F32, tag="wa_raw0")
        nc.gpsimd.memset(grow[:], 0.0)
        for r, g in enumerate((gt, gi)):
            nc.sync.dma_start(
                grow[4 * r : 4 * r + 4, :].rearrange("t (q e) -> t q e", e=8),
                g.rearrange("(q t e) o -> t q (e o)", t=4, e=8),
            )
        page = []
        mem_v = mem.rearrange("(p t) w -> t p w", t=PACK)
        out_v = out.rearrange("(p t) w -> t p w", t=PACK)
        for t, tag in enumerate(("xw", "wa_raw1", "w16_0", "xa_s_raw")):
            pg = sb("page%d" % t, [P, U], F32, tag=tag)
            nc.sync.dma_start(pg[:], mem_v[t])
            page.append(pg)

        def product(i, lhs_c, lhs_s, t, rhs_c, rhs_s):
            acc = bank(i)
            cols = slice(P * t, P * t + P)
            nc.tensor.matmul_mx(
                out=acc[:],
                lhsT=lhs_c[:, cols].bitcast(FP8X4),
                lhsT_scale=lhs_s[:, cols],
                rhs=rhs_c[:].bitcast(FP8X4),
                rhs_scale=rhs_s[:],
                start=True,
                stop=True,
            )
            return acc

        a_acc = [product(t, xa_w, xa_s, t, w_c[0], w_s[0]) for t in range(PACK)]
        a_sb, sig, pa = [], [], []

        def leave_bank(t, tag=None):
            a_t = sb("a%d" % t, [P, H], F32, tag=tag)
            nc.scalar.copy(a_t[:], a_acc[t][:])
            a_sb.append(a_t)

        def gate(t):
            s_t = sb("sig%d" % t, [P, W], F32)
            nc.scalar.activation(s_t[:], a_sb[t][:].indirect(n2_t[:]), ACT.Sigmoid)
            sig.append(s_t)

        def fetch(t):
            p_t = sb("pa%d" % t, [P, W], F32)
            nc.vector.tensor_copy(p_t[:], a_sb[t][:].indirect(n1_t[:]))
            pa.append(p_t)

        def put(t):
            nc.vector.tensor_tensor(a_sb[t][:].indirect(n2_t[:]), pa[t][:], sig[t][:], ALU.mult)

        def weigh(t):
            dst = z_rows[:, t, :].rearrange("p (u m) -> p m u", u=PACK)
            src = a_sb[t][:].rearrange("p (m u) -> p m u", u=PACK)
            if t == 0:
                nc.scalar.activation(dst, src, ACT.Copy, scale=gates[:, t : t + 1])
            else:
                nc.vector.tensor_scalar_mul(dst, src, gates[:, t : t + 1])

        leave_bank(0)
        leave_bank(1)
        gate(0)
        gate(1)
        wb16 = sb("wb16", [P, N, PACK], BF16, tag="xa_w")
        for h in range(2):
            weave("scalar", wb16[:, 256 * h : 256 * h + 256, :], w_raw[2 + h])
        fetch(0)
        fetch(1)
        put(0)
        put(1)
        quantize(w_c[1][:], w_s[1][:], wb16[:])
        leave_bank(2, "warm")
        leave_bank(3, "cold")
        gate(2)
        gate(3)
        gbank = bank(0)
        nc.tensor.transpose(gbank[:, 0:P], grow[:], ident[:])
        gates = sb("gates", [P, 8], F32)
        nc.scalar.copy(gates[:], gbank[:, 0:8])

        z2_rows = sb("z2_rows", [P, PACK, N], BF16)
        for t in range(PACK):
            acc = product(4 + t, xb_w, xb_s, t, w_c[1], w_s[1])
            nc.scalar.activation(z2_rows[:, t, :], acc[:], ACT.Copy, scale=gates[:, 4 + t : 5 + t])
        z2_16 = []
        for h in range(2):
            half = sb("z2_16_%d" % h, [P, 256, PACK], BF16)
            weave("scalar", half[:], z2_rows[:, :, 256 * h : 256 * h + 256])
            z2_16.append(half)

        z_rows = sb("z_rows", [P, PACK, H], BF16, tag="pa1")
        fetch(2)
        fetch(3)
        weigh(0)
        weigh(1)
        put(2)
        put(3)
        weigh(2)

        z2_c = sb("z2_c", [P, N], U32)
        z2_s = sb("z2_s", [P, N], U8)
        weigh(PACK - 1)
        for h in range(2):
            cols = slice(256 * h, 256 * h + 256)
            quantize(z2_c[:, cols], z2_s[:, cols], z2_16[h][:])

        z16 = sb("z16", [P, H, PACK], BF16, tag="z2_16_0")
        z_c = sb("z_c", [P, H], U32)
        z_s = sb("z_s", [P, H], U8)
        for u in range(PACK + 1):
            if u < PACK:
                cols = slice(P * u, P * u + P)
                weave("vector", z16[:, cols, :], z_rows[:, :, cols])
            if u > 0:
                cols = slice(P * (u - 1), P * u)
                quantize(z_c[:, cols], z_s[:, cols], z16[:, cols, :])

        accs, kept = [], []
        for u in range(PACK):
            acc = product(u, z_c, z_s, u, z2_c, z2_s)
            rest = sb("rest%d" % u, [P, N], F32)
            nc.scalar.activation(rest[:], acc[:], ACT.Sigmoid, scale=-0.0625)
            k_u = sb("kept%d" % u, [P, N], F32, tag="z2_16_0" if u == 0 else None)
            nc.vector.tensor_tensor(k_u[:], page[u][:].indirect(n3_t[:]), rest[:], ALU.mult)
            accs.append(acc)
            kept.append(k_u)
        fresh = sb("fresh", [P, PACK, N], F32, tag="z_c")
        for u in range(PACK):
            nc.scalar.activation(fresh[:, u, :], accs[u][:], ACT.Silu, scale=0.0625)
            nc.vector.tensor_tensor(page[u][:].indirect(n3_t[:]), kept[u][:], fresh[:, u, :], ALU.add)
            nc.sync.dma_start(out_v[u], page[u][:])
